import numpy as np
import ml_dtypes


def mxq(x, axis, fmt="e4m3"):
    dtype, down = {"e4m3": (ml_dtypes.float8_e4m3fn, 7), "e5m2": (ml_dtypes.float8_e5m2, 14)}[fmt]
    v = np.moveaxis(np.asarray(x, np.float32).astype(ml_dtypes.bfloat16).astype(np.float64), axis, -1)
    blocks = v.reshape(v.shape[:-1] + (-1, 32))
    amax = np.abs(blocks).max(-1, keepdims=True)
    byte = np.maximum(np.where(amax > 0, np.frexp(amax)[1] - 1 + 127, 0) - down, 1)
    scale = np.exp2(byte - 127.0)
    codes = (blocks / scale).astype(np.float32).astype(dtype).astype(np.float64)
    return np.moveaxis((codes * scale).reshape(v.shape), -1, axis)


WIDE = False


def mx_kscale(k):
    if not WIDE:
        return np.ones(k)
    levels = np.array([10, -10, 5, -5, 0])
    if k % 512:
        return np.exp2(np.random.permutation(np.resize(levels, k // 32))).repeat(32)
    a = np.empty((k // 512, 16))
    for p in range(k // 512):
        a[p, :8] = np.random.permutation(np.resize(levels, 8))
        for g in range(8):
            far = levels[np.abs(levels - a[p, g]) >= 10]
            a[p, g + 8] = far[np.random.randint(len(far))]
    return np.exp2(a.ravel()).repeat(32)


def f64(x):
    return np.asarray(x).astype(np.float64)


def striped8(idx):
    return np.asarray(idx).reshape(8, -1, 16).transpose(0, 2, 1).reshape(128, -1).astype(np.uint16)


def unstriped8(offs):
    return offs.reshape(8, 16, -1).transpose(0, 2, 1).reshape(8, -1).astype(np.int64)


def pick8(x, idx, run):
    r = np.arange(len(x))
    return x[r[:, None], idx[r % (8 * run) // run]]


E2M1 = np.array([0.0, 0.5, 1.0, 1.5, 2.0, 3.0, 4.0, 6.0, -0.0, -0.5, -1.0, -1.5, -2.0, -3.0, -4.0, -6.0])


def pack_weight(w, fmt):
    k, n = w.shape
    w = f64(np.asarray(w, np.float32).astype(ml_dtypes.bfloat16)).reshape(k // 32, 32, n)
    amax = np.abs(w).max(1)
    if fmt == "e4m3":
        byte = np.frexp(amax)[1] - 1 + 127 - 7
    else:
        mant, ex = np.frexp(amax / 6.0)
        byte = np.where(mant > 0.5, ex, ex - 1) + 127
    byte = np.clip(np.where(amax > 0, byte, 1), 1, 254)
    scaled = (w * np.exp2(127.0 - byte)[:, None, :]).reshape(k, n).astype(np.float32)
    by_word = np.ascontiguousarray(scaled.reshape(k // 512, 128, 4, n).transpose(0, 1, 3, 2))
    if fmt == "e4m3":
        words = by_word.astype(ml_dtypes.float8_e4m3fn).view(np.uint8)
    else:
        c = by_word.astype(ml_dtypes.float4_e2m1fn).view(np.uint8) & 0xF
        words = (c[..., 0::2] | (c[..., 1::2] << 4)).reshape(k // 512, 128, 2 * n)
    return np.ascontiguousarray(words), np.ascontiguousarray(byte.astype(np.uint8).reshape(k // 512, 16, n))


def unpack_weight(words, scales, fmt):
    g, _, n = scales.shape
    words = np.ascontiguousarray(words).reshape(g, 128, n, -1)
    if fmt == "e4m3":
        vals = words.view(ml_dtypes.float8_e4m3fn).astype(np.float64)
    else:
        nib = np.empty((g, 128, n, 4), np.uint8)
        nib[..., 0::2] = words & 0xF
        nib[..., 1::2] = words >> 4
        vals = E2M1[nib]
    vals = vals * np.repeat(np.exp2(scales.astype(np.float64) - 127.0), 8, axis=1)[..., None]
    return vals.transpose(0, 1, 3, 2).reshape(g * 512, n)


K, T, J, N, L = 512, 512, 256, 512, 512


def setup_inputs():
    n = np.random.standard_normal
    idx = np.stack([np.random.permutation(T)[:J] for _ in range(8)])
    idx2 = np.stack([np.random.permutation(T)[:J] for _ in range(8)])
    fk = mx_kscale(K)
    fl = mx_kscale(L)
    xtp = pack_weight(n((K, T)) / fk[:, None], "e4m3")
    wp = pack_weight(n((K, N)) * 1 / np.sqrt(K) * fk[:, None], "e2m1")
    wgp = pack_weight(n((L, N)) * 1 / np.sqrt(L) * fl[:, None], "e4m3")
    return {
        "xt_words": xtp[0],
        "xt_scales": xtp[1],
        "w_words": wp[0],
        "w_scales": wp[1],
        "gx": (n((L, J)) / fl[:, None]).astype(np.float32),
        "wg_words": wgp[0],
        "wg_scales": wgp[1],
        "offs": striped8(idx),
        "offs2": striped8(idx2),
    }


def reference(xt_words, xt_scales, w_words, w_scales, gx, wg_words, wg_scales, offs, offs2):
    idx = unstriped8(offs)
    idx2 = unstriped8(offs2)
    xtu = unpack_weight(xt_words, xt_scales, "e4m3")
    wu = unpack_weight(w_words, w_scales, "e2m1")
    wgu = unpack_weight(wg_words, wg_scales, "e4m3")
    z = wu.T @ xtu
    gxq = mxq(f64(gx), 0, "e4m3")
    g = wgu.T @ gxq
    d = pick8(z, idx, 64) * np.tanh(g)
    p = np.zeros((N, T))
    p[np.arange(N)[:, None], idx2[np.arange(N) % 512 // 64]] = d
    y = z + p
    return y

@@ -1,0 +1,140 @@
+from contextlib import ExitStack
+
+import concourse.mybir as mybir
+
+K, T, J, N, L = 512, 512, 256, 512, 512
+FLOPS = 2 * K * N * T + 2 * L * N * J
+
+F32 = mybir.dt.float32
+BF16 = mybir.dt.bfloat16
+I32 = mybir.dt.int32
+U8 = mybir.dt.uint8
+U16 = mybir.dt.uint16
+FP8X4 = mybir.dt.float8_e4m3fn_x4
+FP4X4 = mybir.dt.float4_e2m1fn_x4
+MULT = mybir.AluOpType.mult
+ADD = mybir.AluOpType.add
+TANH = mybir.ActivationFunctionType.Tanh
+
+P = 128
+TILES = 4
+RUNS = 16
+
+
+def load_scale_rows(queue, tile, scales, q):
+    queue.dma_start(out=tile[32 * q : 32 * q + 4, :].bitcast(I32), in_=scales[0, 4 * q : 4 * q + 4, :].bitcast(I32))
+
+
+def deal(nc, dealt, raw):
+    nc.vector.tensor_copy(
+        out=dealt.bitcast(I32).rearrange("p (i q e) -> p i q e", i=TILES, q=RUNS),
+        in_=raw.bitcast(I32).rearrange("p (q i e) -> p i q e", i=TILES, q=RUNS),
+    )
+
+
+def tile_list_head_read_here_write_there_kernel(
+    tc, xt_words, xt_scales, w_words, w_scales, gx, wg_words, wg_scales, offs, offs2, out
+):
+    nc = tc.nc
+    with ExitStack() as ctx:
+        pool = ctx.enter_context(tc.tile_pool(name="pool", bufs=1))
+        psum = ctx.enter_context(tc.psum_pool(name="psum", bufs=1))
+
+        read_list = pool.tile([P, J // 16], U16, name="read_list")
+        write_list = pool.tile([P, J // 16], U16, name="write_list")
+        w_raw = pool.tile([P, 2 * N], U8, name="w_raw", align_bytes=64)
+        w_codes = pool.tile([P, 2 * N], U8, name="w_codes", align_bytes=64)
+        ws_raw = pool.tile([P, N], U8, name="ws_raw", align_bytes=64)
+        ws = pool.tile([P, N], U8, name="ws", align_bytes=64)
+        wg_raw = pool.tile([P, 4 * N], U8, name="wg_raw", align_bytes=64)
+        wg_codes = pool.tile([P, 4 * N], U8, name="wg_codes", align_bytes=64)
+        wgs_raw = pool.tile([P, N], U8, name="wgs_raw", align_bytes=64)
+        wgs = pool.tile([P, N], U8, name="wgs", align_bytes=64)
+        x_codes = pool.tile([P, 4 * T], U8, name="x_codes", align_bytes=64)
+        xs = pool.tile([P, T], U8, name="xs", align_bytes=64)
+        gx_raw = pool.tile([P, 4, J], F32, name="gx_raw", align_bytes=64)
+        gx_bf = pool.tile([P, 4 * J], BF16, name="gx_bf", align_bytes=64)
+        gx_codes = pool.tile([P, 4 * J], U8, name="gx_codes", align_bytes=64)
+        gxs = pool.tile([P, J], U8, name="gxs", align_bytes=64)
+        warm_in = pool.tile([P, 8], F32, name="warm_in")
+        warm_out = pool.tile([P, 8], F32, name="warm_out")
+
+        nc.vector.memset(wgs_raw[:].bitcast(I32), 0)
+        nc.vector.memset(warm_in[:], 0.0)
+        nc.vector.memset(xs[:].bitcast(I32), 0)
+        nc.vector.memset(ws[:].bitcast(I32), 0)
+
+        load_scale_rows(nc.scalar, ws_raw, w_scales, 0)
+        nc.sync.dma_start(out=w_raw[:].bitcast(I32), in_=w_words[0].bitcast(I32))
+        load_scale_rows(nc.scalar, ws_raw, w_scales, 1)
+        nc.sync.dma_start(out=gx_raw[:], in_=gx.rearrange("(p t) j -> p t j", t=4))
+        load_scale_rows(nc.scalar, ws_raw, w_scales, 2)
+        nc.sync.dma_start(out=x_codes[:].bitcast(I32), in_=xt_words[0].rearrange("p c r -> p (c r)").bitcast(I32))
+        load_scale_rows(nc.scalar, ws_raw, w_scales, 3)
+        nc.sync.dma_start(out=wg_raw[:].bitcast(I32), in_=wg_words[0].rearrange("p c r -> p (c r)").bitcast(I32))
+        load_scale_rows(nc.gpsimd, wgs_raw, wg_scales, 2)
+        load_scale_rows(nc.gpsimd, wgs_raw, wg_scales, 3)
+
+        nc.scalar.activation(out=warm_out[:], in_=warm_in[:], func=TANH)
+
+        load_scale_rows(nc.scalar, xs, xt_scales, 0)
+        load_scale_rows(nc.sync, wgs_raw, wg_scales, 0)
+        load_scale_rows(nc.scalar, xs, xt_scales, 1)
+        load_scale_rows(nc.sync, wgs_raw, wg_scales, 1)
+        load_scale_rows(nc.scalar, xs, xt_scales, 2)
+        nc.sync.dma_start(read_list[:], offs)
+        load_scale_rows(nc.scalar, xs, xt_scales, 3)
+        nc.sync.dma_start(write_list[:], offs2)
+
+        pages = []
+        for i in range(TILES):
+            page = pool.tile([P, T], F32, name="page%d" % i)
+            nc.vector.memset(page[:], 0.0)
+            pages.append(page)
+
+        for q in range(4):
+            deal(nc, ws[32 * q : 32 * q + 4, :], ws_raw[32 * q : 32 * q + 4, :])
+        deal(nc, w_codes[:], w_raw[:])
+        nc.vector.tensor_copy(
+            out=gx_bf[:].rearrange("p (c i t) -> p c t i", i=4, t=4),
+            in_=gx_raw[:].rearrange("p t (c i) -> p c t i", i=4),
+        )
+        nc.vector.quantize_mx(out=gx_codes[:].bitcast(FP8X4), scales=gxs[:], in_=gx_bf[:])
+        deal(nc, wg_codes[:], wg_raw[:])
+        deal(nc, wgs[:], wgs_raw[:])
+
+        rows = out.rearrange("(q i e) t -> i q e t", i=TILES, q=RUNS)
+        for i in range(TILES):
+            z_bank = psum.tile([P, T], F32, name="z_bank%d" % i)
+            nc.tensor.matmul_mx(
+                out=z_bank[:],
+                lhsT=w_codes[:, 2 * P * i : 2 * P * (i + 1)].bitcast(FP4X4),
+                lhsT_scale=ws[:, P * i : P * (i + 1)],
+                rhs=x_codes[:].bitcast(FP8X4),
+                rhs_scale=xs[:],
+                start=True,
+                stop=True,
+            )
+            g_bank = psum.tile([P, J], F32, name="g_bank%d" % i)
+            nc.tensor.matmul_mx(
+                out=g_bank[:],
+                lhsT=wg_codes[:, 4 * P * i : 4 * P * (i + 1)].bitcast(FP8X4),
+                lhsT_scale=wgs[:, P * i : P * (i + 1)],
+                rhs=gx_codes[:].bitcast(FP8X4),
+                rhs_scale=gxs[:],
+                start=True,
+                stop=True,
+            )
+            z = pool.tile([P, T], F32, name="z%d" % i)
+            nc.scalar.copy(out=z[:], in_=z_bank[:])
+            gate = pool.tile([P, J], F32, name="gate%d" % i)
+            nc.scalar.activation(out=gate[:], in_=g_bank[:], func=TANH)
+            d = pool.tile([P, J], F32, name="d%d" % i)
+            nc.vector.tensor_tensor(d[:], z[:].indirect(read_list[:]), gate[:], MULT)
+            nc.vector.tensor_copy(pages[i][:].indirect(write_list[:]), d[:])
+            y = pool.tile([P, T], F32, name="y%d" % i)
+            if i < TILES - 1:
+                nc.gpsimd.tensor_tensor(y[:], z[:], pages[i][:], ADD)
+            else:
+                nc.vector.tensor_tensor(y[:], z_bank[:], pages[i][:], ADD)
+            nc.sync.dma_start(out=rows[i], in_=y[:])

@@ -1,6 +1,7 @@
 from contextlib import ExitStack
 
 import concourse.mybir as mybir
+from concourse.masks import make_identity
 
 K, T, J, N, L = 512, 512, 256, 512, 512
 FLOPS = 2 * K * N * T + 2 * L * N * J
@@ -19,6 +20,8 @@ TANH = mybir.ActivationFunctionType.Tanh
 P = 128
 TILES = 4
 RUNS = 16
+SPLIT = 128
+PE_TILES = 2
 
 
 def load_scale_rows(queue, tile, scales, q):
@@ -46,9 +49,9 @@ def tile_list_head_read_here_write_there_kernel(
         w_codes = pool.tile([P, 2 * N], U8, name="w_codes", align_bytes=64)
         ws_raw = pool.tile([P, N], U8, name="ws_raw", align_bytes=64)
         ws = pool.tile([P, N], U8, name="ws", align_bytes=64)
-        wg_raw = pool.tile([P, 4 * N], U8, name="wg_raw", align_bytes=64)
+        wg_raw = pool.tile([P, 4 * N], U8, name="wg_raw", tag="picked0", align_bytes=64)
         wg_codes = pool.tile([P, 4 * N], U8, name="wg_codes", align_bytes=64)
-        wgs_raw = pool.tile([P, N], U8, name="wgs_raw", align_bytes=64)
+        wgs_raw = pool.tile([P, N], U8, name="wgs_raw", tag="picked1", align_bytes=64)
         wgs = pool.tile([P, N], U8, name="wgs", align_bytes=64)
         x_codes = pool.tile([P, 4 * T], U8, name="x_codes", align_bytes=64)
         xs = pool.tile([P, T], U8, name="xs", align_bytes=64)
@@ -59,63 +62,79 @@ def tile_list_head_read_here_write_there_kernel(
         warm_in = pool.tile([P, 8], F32, name="warm_in")
         warm_out = pool.tile([P, 8], F32, name="warm_out")
 
-        nc.vector.memset(wgs_raw[:].bitcast(I32), 0)
-        nc.vector.memset(warm_in[:], 0.0)
         nc.vector.memset(xs[:].bitcast(I32), 0)
+        nc.vector.memset(warm_in[:], 0.0)
         nc.vector.memset(ws[:].bitcast(I32), 0)
-
-        load_scale_rows(nc.scalar, ws_raw, w_scales, 0)
-        nc.sync.dma_start(out=w_raw[:].bitcast(I32), in_=w_words[0].bitcast(I32))
-        load_scale_rows(nc.scalar, ws_raw, w_scales, 1)
-        nc.sync.dma_start(out=gx_raw[:], in_=gx.rearrange("(p t) j -> p t j", t=4))
-        load_scale_rows(nc.scalar, ws_raw, w_scales, 2)
-        nc.sync.dma_start(out=x_codes[:].bitcast(I32), in_=xt_words[0].rearrange("p c r -> p (c r)").bitcast(I32))
-        load_scale_rows(nc.scalar, ws_raw, w_scales, 3)
-        nc.sync.dma_start(out=wg_raw[:].bitcast(I32), in_=wg_words[0].rearrange("p c r -> p (c r)").bitcast(I32))
-        load_scale_rows(nc.gpsimd, wgs_raw, wg_scales, 2)
-        load_scale_rows(nc.gpsimd, wgs_raw, wg_scales, 3)
-
-        nc.scalar.activation(out=warm_out[:], in_=warm_in[:], func=TANH)
-
-        load_scale_rows(nc.scalar, xs, xt_scales, 0)
-        load_scale_rows(nc.sync, wgs_raw, wg_scales, 0)
-        load_scale_rows(nc.scalar, xs, xt_scales, 1)
-        load_scale_rows(nc.sync, wgs_raw, wg_scales, 1)
-        load_scale_rows(nc.scalar, xs, xt_scales, 2)
-        nc.sync.dma_start(read_list[:], offs)
-        load_scale_rows(nc.scalar, xs, xt_scales, 3)
-        nc.sync.dma_start(write_list[:], offs2)
-
         pages = []
         for i in range(TILES):
             page = pool.tile([P, T], F32, name="page%d" % i)
             nc.vector.memset(page[:], 0.0)
             pages.append(page)
 
+        nc.gpsimd.memset(wgs_raw[:].bitcast(I32), 0)
+        for q in range(2):
+            load_scale_rows(nc.gpsimd, wgs_raw, wg_scales, q)
+        for q in range(4):
+            load_scale_rows(nc.sync if q % 2 else nc.scalar, ws_raw, w_scales, q)
+        load_scale_rows(nc.scalar, xs, xt_scales, 0)
+        nc.sync.dma_start(out=w_raw[:].bitcast(I32), in_=w_words[0].bitcast(I32))
+        nc.sync.dma_start(out=gx_raw[:], in_=gx.rearrange("(p t) j -> p t j", t=4))
+        nc.sync.dma_start(out=x_codes[:].bitcast(I32), in_=xt_words[0].rearrange("p c r -> p (c r)").bitcast(I32))
+        for q in range(1, 4):
+            load_scale_rows(nc.sync, xs, xt_scales, q)
+        nc.sync.dma_start(read_list[:], offs)
+        nc.sync.dma_start(out=wg_raw[:].bitcast(I32), in_=wg_words[0].rearrange("p c r -> p (c r)").bitcast(I32))
+        for q in range(2, 4):
+            load_scale_rows(nc.sync, wgs_raw, wg_scales, q)
+        nc.sync.dma_start(write_list[:], offs2)
+
+        nc.scalar.activation(out=warm_out[:], in_=warm_in[:], func=TANH)
+        ident = pool.tile([P, P], F32, name="ident")
+        nc.vector.memset(ident[:], 0.0)
+        make_identity(nc, ident[:], nomemset=True)
+
         for q in range(4):
             deal(nc, ws[32 * q : 32 * q + 4, :], ws_raw[32 * q : 32 * q + 4, :])
         deal(nc, w_codes[:], w_raw[:])
-        nc.vector.tensor_copy(
-            out=gx_bf[:].rearrange("p (c i t) -> p c t i", i=4, t=4),
-            in_=gx_raw[:].rearrange("p t (c i) -> p c t i", i=4),
-        )
+        for copy, lo, hi in ((nc.vector.tensor_copy, 0, SPLIT), (nc.scalar.copy, SPLIT, J)):
+            copy(
+                out=gx_bf[:, 4 * lo : 4 * hi].rearrange("p (c i t) -> p c t i", i=4, t=4),
+                in_=gx_raw[:, :, lo:hi].rearrange("p t (c i) -> p c t i", i=4),
+            )
         nc.vector.quantize_mx(out=gx_codes[:].bitcast(FP8X4), scales=gxs[:], in_=gx_bf[:])
         deal(nc, wg_codes[:], wg_raw[:])
         deal(nc, wgs[:], wgs_raw[:])
 
         rows = out.rearrange("(q i e) t -> i q e t", i=TILES, q=RUNS)
-        for i in range(TILES):
-            z_bank = psum.tile([P, T], F32, name="z_bank%d" % i)
-            nc.tensor.matmul_mx(
-                out=z_bank[:],
-                lhsT=w_codes[:, 2 * P * i : 2 * P * (i + 1)].bitcast(FP4X4),
-                lhsT_scale=ws[:, P * i : P * (i + 1)],
-                rhs=x_codes[:].bitcast(FP8X4),
-                rhs_scale=xs[:],
-                start=True,
-                stop=True,
-            )
-            g_bank = psum.tile([P, J], F32, name="g_bank%d" % i)
+        zs, picked = [], []
+
+        def turn(bank, tile, c, start, stop):
+            cols = slice(P * c, P * (c + 1))
+            nc.tensor.matmul(bank[:, cols], tile[:, cols], ident[:], start=start, stop=stop, is_transpose=True)
+
+        def features(i):
+            z = pool.tile([P, T], F32, name="z%d" % i)
+            parts = 2 if i == 0 else 1
+            for h in range(parts):
+                lo, hi = h * T // parts, (h + 1) * T // parts
+                bank = psum.tile([P, hi - lo], F32, name="z_bank%d_%d" % (i, h), tag="bank%d_%d" % (i, h))
+                nc.tensor.matmul_mx(
+                    out=bank[:],
+                    lhsT=w_codes[:, 2 * P * i : 2 * P * (i + 1)].bitcast(FP4X4),
+                    lhsT_scale=ws[:, P * i : P * (i + 1)],
+                    rhs=x_codes[:, 4 * lo : 4 * hi].bitcast(FP8X4),
+                    rhs_scale=xs[:, lo:hi],
+                    start=True,
+                    stop=True,
+                )
+                nc.scalar.copy(out=z[:, lo:hi], in_=bank[:])
+            zs.append(z)
+            gz = pool.tile([P, J], F32, name="picked%d" % i, tag="picked%d" % i, align_bytes=64)
+            nc.vector.tensor_copy(gz[:], z[:].indirect(read_list[:]))
+            picked.append(gz)
+
+        def place(i):
+            g_bank = psum.tile([P, J], F32, name="g_bank%d" % i, tag="bank%d_0" % min(i + 1, TILES - 1))
             nc.tensor.matmul_mx(
                 out=g_bank[:],
                 lhsT=wg_codes[:, 4 * P * i : 4 * P * (i + 1)].bitcast(FP8X4),
@@ -125,16 +144,29 @@ def tile_list_head_read_here_write_there_kernel(
                 start=True,
                 stop=True,
             )
-            z = pool.tile([P, T], F32, name="z%d" % i)
-            nc.scalar.copy(out=z[:], in_=z_bank[:])
             gate = pool.tile([P, J], F32, name="gate%d" % i)
             nc.scalar.activation(out=gate[:], in_=g_bank[:], func=TANH)
-            d = pool.tile([P, J], F32, name="d%d" % i)
-            nc.vector.tensor_tensor(d[:], z[:].indirect(read_list[:]), gate[:], MULT)
-            nc.vector.tensor_copy(pages[i][:].indirect(write_list[:]), d[:])
             y = pool.tile([P, T], F32, name="y%d" % i)
-            if i < TILES - 1:
-                nc.gpsimd.tensor_tensor(y[:], z[:], pages[i][:], ADD)
+            nc.vector.tensor_tensor(pages[i][:].indirect(write_list[:]), picked[i][:], gate[:], MULT)
+            if i < PE_TILES:
+                total = psum.tile([P, T], F32, name="total%d" % i, tag="bank1_0")
+                for c in range(4):
+                    turn(total, zs[i], c, c == 0, False)
+                for c in range(4):
+                    turn(total, pages[i], c, False, c == 3)
+                turned = pool.tile([P, T], F32, name="turned%d" % i)
+                nc.scalar.copy(out=turned[:], in_=total[:])
+                back = psum.tile([P, T], F32, name="back")
+                for c in range(4):
+                    turn(back, turned, c, c == 0, c == 3)
+                nc.scalar.copy(out=y[:], in_=back[:])
+                nc.scalar.dma_start(out=rows[i], in_=y[:])
             else:
-                nc.vector.tensor_tensor(y[:], z_bank[:], pages[i][:], ADD)
-            nc.sync.dma_start(out=rows[i], in_=y[:])
+                nc.vector.tensor_tensor(y[:], zs[i][:], pages[i][:], ADD)
+                nc.sync.dma_start(out=rows[i], in_=y[:])
+
+        features(0)
+        for i in range(TILES):
+            if i + 1 < TILES:
+                features(i + 1)
+            place(i)

@@ -21,7 +21,6 @@ P = 128
 TILES = 4
 RUNS = 16
 SPLIT = 128
-PE_TILES = 2
 
 
 def load_scale_rows(queue, tile, scales, q):
@@ -49,9 +48,9 @@ def tile_list_head_read_here_write_there_kernel(
         w_codes = pool.tile([P, 2 * N], U8, name="w_codes", align_bytes=64)
         ws_raw = pool.tile([P, N], U8, name="ws_raw", align_bytes=64)
         ws = pool.tile([P, N], U8, name="ws", align_bytes=64)
-        wg_raw = pool.tile([P, 4 * N], U8, name="wg_raw", tag="picked0", align_bytes=64)
+        gate_raw = pool.tile([P, 5 * N], U8, name="gate_raw", tag="picked0", align_bytes=64)
+        wg_raw, wgs_raw = gate_raw[:, : 4 * N], gate_raw[:, 4 * N :]
         wg_codes = pool.tile([P, 4 * N], U8, name="wg_codes", align_bytes=64)
-        wgs_raw = pool.tile([P, N], U8, name="wgs_raw", tag="picked1", align_bytes=64)
         wgs = pool.tile([P, N], U8, name="wgs", align_bytes=64)
         x_codes = pool.tile([P, 4 * T], U8, name="x_codes", align_bytes=64)
         xs = pool.tile([P, T], U8, name="xs", align_bytes=64)
@@ -71,7 +70,7 @@ def tile_list_head_read_here_write_there_kernel(
             nc.vector.memset(page[:], 0.0)
             pages.append(page)
 
-        nc.gpsimd.memset(wgs_raw[:].bitcast(I32), 0)
+        nc.gpsimd.memset(wgs_raw.bitcast(I32), 0)
         for q in range(2):
             load_scale_rows(nc.gpsimd, wgs_raw, wg_scales, q)
         for q in range(4):
@@ -83,7 +82,7 @@ def tile_list_head_read_here_write_there_kernel(
         for q in range(1, 4):
             load_scale_rows(nc.sync, xs, xt_scales, q)
         nc.sync.dma_start(read_list[:], offs)
-        nc.sync.dma_start(out=wg_raw[:].bitcast(I32), in_=wg_words[0].rearrange("p c r -> p (c r)").bitcast(I32))
+        nc.sync.dma_start(out=wg_raw.bitcast(I32), in_=wg_words[0].rearrange("p c r -> p (c r)").bitcast(I32))
         for q in range(2, 4):
             load_scale_rows(nc.sync, wgs_raw, wg_scales, q)
         nc.sync.dma_start(write_list[:], offs2)
@@ -102,11 +101,12 @@ def tile_list_head_read_here_write_there_kernel(
                 in_=gx_raw[:, :, lo:hi].rearrange("p t (c i) -> p c t i", i=4),
             )
         nc.vector.quantize_mx(out=gx_codes[:].bitcast(FP8X4), scales=gxs[:], in_=gx_bf[:])
-        deal(nc, wg_codes[:], wg_raw[:])
-        deal(nc, wgs[:], wgs_raw[:])
+        deal(nc, wg_codes[:], wg_raw)
+        deal(nc, wgs[:], wgs_raw)
 
         rows = out.rearrange("(q i e) t -> i q e t", i=TILES, q=RUNS)
-        zs, picked = [], []
+        zs = []
+        picked = pool.tile([P, 3, J], F32, name="picked", tag="picked0", align_bytes=64)
 
         def turn(bank, tile, c, start, stop):
             cols = slice(P * c, P * (c + 1))
@@ -129,12 +129,9 @@ def tile_list_head_read_here_write_there_kernel(
                 )
                 nc.scalar.copy(out=z[:, lo:hi], in_=bank[:])
             zs.append(z)
-            gz = pool.tile([P, J], F32, name="picked%d" % i, tag="picked%d" % i, align_bytes=64)
-            nc.vector.tensor_copy(gz[:], z[:].indirect(read_list[:]))
-            picked.append(gz)
 
-        def place(i):
-            g_bank = psum.tile([P, J], F32, name="g_bank%d" % i, tag="bank%d_0" % min(i + 1, TILES - 1))
+        def gate(i, bank_tag):
+            g_bank = psum.tile([P, J], F32, name="g_bank%d" % i, tag=bank_tag)
             nc.tensor.matmul_mx(
                 out=g_bank[:],
                 lhsT=wg_codes[:, 4 * P * i : 4 * P * (i + 1)].bitcast(FP8X4),
@@ -144,29 +141,49 @@ def tile_list_head_read_here_write_there_kernel(
                 start=True,
                 stop=True,
             )
-            gate = pool.tile([P, J], F32, name="gate%d" % i)
-            nc.scalar.activation(out=gate[:], in_=g_bank[:], func=TANH)
+            tanh_g = pool.tile([P, J], F32, name="tanh_g%d" % i)
+            nc.scalar.activation(out=tanh_g[:], in_=g_bank[:], func=TANH)
+            return tanh_g
+
+        def pick(i):
+            nc.vector.tensor_copy(picked[:, i, :], zs[i][:].indirect(read_list[:]))
+
+        def place(i):
+            tanh_g = gate(i, "bank%d_0" % (i + 1))
+            nc.vector.tensor_tensor(pages[i][:].indirect(write_list[:]), picked[:, i, :], tanh_g[:], MULT)
+
+        def sum_by_turns(i):
+            total = psum.tile([P, T], F32, name="total%d" % i, tag="bank%d_0" % (i + 1))
+            for c in range(4):
+                turn(total, zs[i], c, c == 0, False)
+            for c in range(4):
+                turn(total, pages[i], c, False, c == 3)
+            turned = pool.tile([P, T], F32, name="turned%d" % i)
+            nc.scalar.copy(out=turned[:], in_=total[:])
+            back = psum.tile([P, T], F32, name="back%d" % i)
+            for c in range(4):
+                turn(back, turned, c, c == 0, c == 3)
             y = pool.tile([P, T], F32, name="y%d" % i)
-            nc.vector.tensor_tensor(pages[i][:].indirect(write_list[:]), picked[i][:], gate[:], MULT)
-            if i < PE_TILES:
-                total = psum.tile([P, T], F32, name="total%d" % i, tag="bank1_0")
-                for c in range(4):
-                    turn(total, zs[i], c, c == 0, False)
-                for c in range(4):
-                    turn(total, pages[i], c, False, c == 3)
-                turned = pool.tile([P, T], F32, name="turned%d" % i)
-                nc.scalar.copy(out=turned[:], in_=total[:])
-                back = psum.tile([P, T], F32, name="back")
-                for c in range(4):
-                    turn(back, turned, c, c == 0, c == 3)
-                nc.scalar.copy(out=y[:], in_=back[:])
-                nc.scalar.dma_start(out=rows[i], in_=y[:])
-            else:
-                nc.vector.tensor_tensor(y[:], zs[i][:], pages[i][:], ADD)
-                nc.sync.dma_start(out=rows[i], in_=y[:])
+            nc.scalar.copy(out=y[:], in_=back[:])
+            nc.scalar.dma_start(out=rows[i], in_=y[:])
 
         features(0)
-        for i in range(TILES):
-            if i + 1 < TILES:
-                features(i + 1)
+        pick(0)
+        for i in range(2):
+            features(i + 1)
+            pick(i + 1)
             place(i)
+            sum_by_turns(i)
+        features(3)
+        place(2)
+        y2 = pool.tile([P, T], F32, name="y2")
+        nc.gpsimd.tensor_tensor(y2[:], zs[2][:], pages[2][:], ADD)
+        nc.sync.dma_start(out=rows[2], in_=y2[:])
+        d = pool.tile([P, J], F32, name="d")
+        nc.vector.tensor_tensor(d[:], zs[3][:].indirect(read_list[:]), gate(3, "bank3_0")[:], MULT)
+        nc.vector.tensor_copy(pages[3][:].indirect(write_list[:]), d[:])
+        y3 = pool.tile([P, T], F32, name="y3")
+        for h, queue in enumerate((nc.sync, nc.scalar)):
+            cols = slice(h * T // 2, (h + 1) * T // 2)
+            nc.vector.tensor_tensor(y3[:, cols], zs[3][:, cols], pages[3][:, cols], ADD)
+            queue.dma_start(out=rows[3][:, :, cols], in_=y3[:, cols])

@@ -112,12 +112,12 @@ def tile_list_head_read_here_write_there_kernel(
             cols = slice(P * c, P * (c + 1))
             nc.tensor.matmul(bank[:, cols], tile[:, cols], ident[:], start=start, stop=stop, is_transpose=True)
 
-        def features(i):
-            z = pool.tile([P, T], F32, name="z%d" % i)
-            parts = 2 if i == 0 else 1
+        def features(i, banks):
+            z = pool.tile([P, T], F32, name="z%d" % i, tag="z%d" % i)
+            parts = len(banks)
             for h in range(parts):
                 lo, hi = h * T // parts, (h + 1) * T // parts
-                bank = psum.tile([P, hi - lo], F32, name="z_bank%d_%d" % (i, h), tag="bank%d_%d" % (i, h))
+                bank = psum.tile([P, hi - lo], F32, name="z_bank%d_%d" % (i, h), tag=banks[h])
                 nc.tensor.matmul_mx(
                     out=bank[:],
                     lhsT=w_codes[:, 2 * P * i : 2 * P * (i + 1)].bitcast(FP4X4),
@@ -149,11 +149,10 @@ def tile_list_head_read_here_write_there_kernel(
             nc.vector.tensor_copy(picked[:, i, :], zs[i][:].indirect(read_list[:]))
 
         def place(i):
-            tanh_g = gate(i, "bank%d_0" % (i + 1))
-            nc.vector.tensor_tensor(pages[i][:].indirect(write_list[:]), picked[:, i, :], tanh_g[:], MULT)
+            nc.vector.tensor_tensor(pages[i][:].indirect(write_list[:]), picked[:, i, :], gates[i][:], MULT)
 
         def sum_by_turns(i):
-            total = psum.tile([P, T], F32, name="total%d" % i, tag="bank%d_0" % (i + 1))
+            total = psum.tile([P, T], F32, name="total%d" % i, tag="BC"[i])
             for c in range(4):
                 turn(total, zs[i], c, c == 0, False)
             for c in range(4):
@@ -167,23 +166,23 @@ def tile_list_head_read_here_write_there_kernel(
             nc.scalar.copy(out=y[:], in_=back[:])
             nc.scalar.dma_start(out=rows[i], in_=y[:])
 
-        features(0)
-        pick(0)
+        for i, banks in enumerate(("AB", "C", "D")):
+            features(i, banks)
+            pick(i)
+        gates = [gate(i, "ABCD"[i]) for i in range(TILES)]
+        features(3, "A")
         for i in range(2):
-            features(i + 1)
-            pick(i + 1)
             place(i)
             sum_by_turns(i)
-        features(3)
         place(2)
         y2 = pool.tile([P, T], F32, name="y2")
         nc.gpsimd.tensor_tensor(y2[:], zs[2][:], pages[2][:], ADD)
         nc.sync.dma_start(out=rows[2], in_=y2[:])
         d = pool.tile([P, J], F32, name="d")
-        nc.vector.tensor_tensor(d[:], zs[3][:].indirect(read_list[:]), gate(3, "bank3_0")[:], MULT)
+        nc.vector.tensor_tensor(d[:], zs[3][:].indirect(read_list[:]), gates[3][:], MULT)
         nc.vector.tensor_copy(pages[3][:].indirect(write_list[:]), d[:])
-        y3 = pool.tile([P, T], F32, name="y3")
-        for h, queue in enumerate((nc.sync, nc.scalar)):
+        y3 = pool.tile([P, T], F32, name="y3", tag="z2")
+        for h in range(2):
             cols = slice(h * T // 2, (h + 1) * T // 2)
             nc.vector.tensor_tensor(y3[:, cols], zs[3][:, cols], pages[3][:, cols], ADD)
-            queue.dma_start(out=rows[3][:, :, cols], in_=y3[:, cols])
+            nc.sync.dma_start(out=rows[3][:, :, cols], in_=y3[:, cols])

@@ -81,10 +81,10 @@ def tile_list_head_read_here_write_there_kernel(
         nc.sync.dma_start(out=x_codes[:].bitcast(I32), in_=xt_words[0].rearrange("p c r -> p (c r)").bitcast(I32))
         for q in range(1, 4):
             load_scale_rows(nc.sync, xs, xt_scales, q)
-        nc.sync.dma_start(read_list[:], offs)
         nc.sync.dma_start(out=wg_raw.bitcast(I32), in_=wg_words[0].rearrange("p c r -> p (c r)").bitcast(I32))
         for q in range(2, 4):
             load_scale_rows(nc.sync, wgs_raw, wg_scales, q)
+        nc.sync.dma_start(read_list[:], offs)
         nc.sync.dma_start(write_list[:], offs2)
 
         nc.scalar.activation(out=warm_out[:], in_=warm_in[:], func=TANH)

from contextlib import ExitStack

import concourse.mybir as mybir
from concourse.masks import make_identity

K, T, J, N, L = 512, 512, 256, 512, 512
FLOPS = 2 * K * N * T + 2 * L * N * J

F32 = mybir.dt.float32
BF16 = mybir.dt.bfloat16
I32 = mybir.dt.int32
U8 = mybir.dt.uint8
U16 = mybir.dt.uint16
FP8X4 = mybir.dt.float8_e4m3fn_x4
FP4X4 = mybir.dt.float4_e2m1fn_x4
MULT = mybir.AluOpType.mult
ADD = mybir.AluOpType.add
TANH = mybir.ActivationFunctionType.Tanh

P = 128
TILES = 4
RUNS = 16
SPLIT = 128


def load_scale_rows(queue, tile, scales, q):
    queue.dma_start(out=tile[32 * q : 32 * q + 4, :].bitcast(I32), in_=scales[0, 4 * q : 4 * q + 4, :].bitcast(I32))


def deal(nc, dealt, raw):
    nc.vector.tensor_copy(
        out=dealt.bitcast(I32).rearrange("p (i q e) -> p i q e", i=TILES, q=RUNS),
        in_=raw.bitcast(I32).rearrange("p (q i e) -> p i q e", i=TILES, q=RUNS),
    )


def tile_list_head_read_here_write_there_kernel(
    tc, xt_words, xt_scales, w_words, w_scales, gx, wg_words, wg_scales, offs, offs2, out
):
    nc = tc.nc
    with ExitStack() as ctx:
        pool = ctx.enter_context(tc.tile_pool(name="pool", bufs=1))
        psum = ctx.enter_context(tc.psum_pool(name="psum", bufs=1))

        read_list = pool.tile([P, J // 16], U16, name="read_list")
        write_list = pool.tile([P, J // 16], U16, name="write_list")
        w_raw = pool.tile([P, 2 * N], U8, name="w_raw", align_bytes=64)
        w_codes = pool.tile([P, 2 * N], U8, name="w_codes", align_bytes=64)
        ws_raw = pool.tile([P, N], U8, name="ws_raw", align_bytes=64)
        ws = pool.tile([P, N], U8, name="ws", align_bytes=64)
        gate_raw = pool.tile([P, 5 * N], U8, name="gate_raw", tag="picked0", align_bytes=64)
        wg_raw, wgs_raw = gate_raw[:, : 4 * N], gate_raw[:, 4 * N :]
        wg_codes = pool.tile([P, 4 * N], U8, name="wg_codes", align_bytes=64)
        wgs = pool.tile([P, N], U8, name="wgs", align_bytes=64)
        x_codes = pool.tile([P, 4 * T], U8, name="x_codes", align_bytes=64)
        xs = pool.tile([P, T], U8, name="xs", align_bytes=64)
        gx_raw = pool.tile([P, 4, J], F32, name="gx_raw", align_bytes=64)
        gx_bf = pool.tile([P, 4 * J], BF16, name="gx_bf", align_bytes=64)
        gx_codes = pool.tile([P, 4 * J], U8, name="gx_codes", align_bytes=64)
        gxs = pool.tile([P, J], U8, name="gxs", align_bytes=64)
        warm_in = pool.tile([P, 8], F32, name="warm_in")
        warm_out = pool.tile([P, 8], F32, name="warm_out")

        nc.vector.memset(xs[:].bitcast(I32), 0)
        nc.vector.memset(warm_in[:], 0.0)
        nc.vector.memset(ws[:].bitcast(I32), 0)
        pages = []
        for i in range(TILES):
            page = pool.tile([P, T], F32, name="page%d" % i)
            nc.vector.memset(page[:], 0.0)
            pages.append(page)

        nc.gpsimd.memset(wgs_raw.bitcast(I32), 0)
        for q in range(2):
            load_scale_rows(nc.gpsimd, wgs_raw, wg_scales, q)
        for q in range(4):
            load_scale_rows(nc.sync if q % 2 else nc.scalar, ws_raw, w_scales, q)
        load_scale_rows(nc.scalar, xs, xt_scales, 0)
        nc.sync.dma_start(out=w_raw[:].bitcast(I32), in_=w_words[0].bitcast(I32))
        nc.sync.dma_start(out=gx_raw[:], in_=gx.rearrange("(p t) j -> p t j", t=4))
        nc.sync.dma_start(out=x_codes[:].bitcast(I32), in_=xt_words[0].rearrange("p c r -> p (c r)").bitcast(I32))
        for q in range(1, 4):
            load_scale_rows(nc.sync, xs, xt_scales, q)
        nc.sync.dma_start(out=wg_raw.bitcast(I32), in_=wg_words[0].rearrange("p c r -> p (c r)").bitcast(I32))
        for q in range(2, 4):
            load_scale_rows(nc.sync, wgs_raw, wg_scales, q)
        nc.sync.dma_start(read_list[:], offs)
        nc.sync.dma_start(write_list[:], offs2)

        nc.scalar.activation(out=warm_out[:], in_=warm_in[:], func=TANH)
        ident = pool.tile([P, P], F32, name="ident")
        nc.vector.memset(ident[:], 0.0)
        make_identity(nc, ident[:], nomemset=True)

        for q in range(4):
            deal(nc, ws[32 * q : 32 * q + 4, :], ws_raw[32 * q : 32 * q + 4, :])
        deal(nc, w_codes[:], w_raw[:])
        for copy, lo, hi in ((nc.vector.tensor_copy, 0, SPLIT), (nc.scalar.copy, SPLIT, J)):
            copy(
                out=gx_bf[:, 4 * lo : 4 * hi].rearrange("p (c i t) -> p c t i", i=4, t=4),
                in_=gx_raw[:, :, lo:hi].rearrange("p t (c i) -> p c t i", i=4),
            )
        nc.vector.quantize_mx(out=gx_codes[:].bitcast(FP8X4), scales=gxs[:], in_=gx_bf[:])
        deal(nc, wg_codes[:], wg_raw)
        deal(nc, wgs[:], wgs_raw)

        rows = out.rearrange("(q i e) t -> i q e t", i=TILES, q=RUNS)
        zs = []
        picked = pool.tile([P, 3, J], F32, name="picked", tag="picked0", align_bytes=64)

        def turn(bank, tile, c, start, stop):
            cols = slice(P * c, P * (c + 1))
            nc.tensor.matmul(bank[:, cols], tile[:, cols], ident[:], start=start, stop=stop, is_transpose=True)

        def features(i, banks):
            z = pool.tile([P, T], F32, name="z%d" % i, tag="z%d" % i)
            parts = len(banks)
            for h in range(parts):
                lo, hi = h * T // parts, (h + 1) * T // parts
                bank = psum.tile([P, hi - lo], F32, name="z_bank%d_%d" % (i, h), tag=banks[h])
                nc.tensor.matmul_mx(
                    out=bank[:],
                    lhsT=w_codes[:, 2 * P * i : 2 * P * (i + 1)].bitcast(FP4X4),
                    lhsT_scale=ws[:, P * i : P * (i + 1)],
                    rhs=x_codes[:, 4 * lo : 4 * hi].bitcast(FP8X4),
                    rhs_scale=xs[:, lo:hi],
                    start=True,
                    stop=True,
                )
                nc.scalar.copy(out=z[:, lo:hi], in_=bank[:])
            zs.append(z)

        def gate(i, bank_tag):
            g_bank = psum.tile([P, J], F32, name="g_bank%d" % i, tag=bank_tag)
            nc.tensor.matmul_mx(
                out=g_bank[:],
                lhsT=wg_codes[:, 4 * P * i : 4 * P * (i + 1)].bitcast(FP8X4),
                lhsT_scale=wgs[:, P * i : P * (i + 1)],
                rhs=gx_codes[:].bitcast(FP8X4),
                rhs_scale=gxs[:],
                start=True,
                stop=True,
            )
            tanh_g = pool.tile([P, J], F32, name="tanh_g%d" % i)
            nc.scalar.activation(out=tanh_g[:], in_=g_bank[:], func=TANH)
            return tanh_g

        def pick(i):
            nc.vector.tensor_copy(picked[:, i, :], zs[i][:].indirect(read_list[:]))

        def place(i):
            nc.vector.tensor_tensor(pages[i][:].indirect(write_list[:]), picked[:, i, :], gates[i][:], MULT)

        def sum_by_turns(i):
            total = psum.tile([P, T], F32, name="total%d" % i, tag="BC"[i])
            for c in range(4):
                turn(total, zs[i], c, c == 0, False)
            for c in range(4):
                turn(total, pages[i], c, False, c == 3)
            turned = pool.tile([P, T], F32, name="turned%d" % i)
            nc.scalar.copy(out=turned[:], in_=total[:])
            back = psum.tile([P, T], F32, name="back%d" % i)
            for c in range(4):
                turn(back, turned, c, c == 0, c == 3)
            y = pool.tile([P, T], F32, name="y%d" % i)
            nc.scalar.copy(out=y[:], in_=back[:])
            nc.scalar.dma_start(out=rows[i], in_=y[:])

        for i, banks in enumerate(("AB", "C", "D")):
            features(i, banks)
            pick(i)
        gates = [gate(i, "ABCD"[i]) for i in range(TILES)]
        features(3, "A")
        for i in range(2):
            place(i)
            sum_by_turns(i)
        place(2)
        y2 = pool.tile([P, T], F32, name="y2")
        nc.gpsimd.tensor_tensor(y2[:], zs[2][:], pages[2][:], ADD)
        nc.sync.dma_start(out=rows[2], in_=y2[:])
        d = pool.tile([P, J], F32, name="d")
        nc.vector.tensor_tensor(d[:], zs[3][:].indirect(read_list[:]), gates[3][:], MULT)
        nc.vector.tensor_copy(pages[3][:].indirect(write_list[:]), d[:])
        y3 = pool.tile([P, T], F32, name="y3", tag="z2")
        for h in range(2):
            cols = slice(h * T // 2, (h + 1) * T // 2)
            nc.vector.tensor_tensor(y3[:, cols], zs[3][:, cols], pages[3][:, cols], ADD)
            nc.sync.dma_start(out=rows[3][:, :, cols], in_=y3[:, cols])
